import numpy as np
import ml_dtypes


def mxq(x, axis, fmt="e4m3"):
    dtype, down = {"e4m3": (ml_dtypes.float8_e4m3fn, 7), "e5m2": (ml_dtypes.float8_e5m2, 14)}[fmt]
    v = np.moveaxis(np.asarray(x, np.float32).astype(ml_dtypes.bfloat16).astype(np.float64), axis, -1)
    blocks = v.reshape(v.shape[:-1] + (-1, 32))
    amax = np.abs(blocks).max(-1, keepdims=True)
    byte = np.maximum(np.where(amax > 0, np.frexp(amax)[1] - 1 + 127, 0) - down, 1)
    scale = np.exp2(byte - 127.0)
    codes = (blocks / scale).astype(np.float32).astype(dtype).astype(np.float64)
    return np.moveaxis((codes * scale).reshape(v.shape), -1, axis)


WIDE = False


def mx_kscale(k):
    if not WIDE:
        return np.ones(k)
    levels = np.array([10, -10, 5, -5, 0])
    if k % 512:
        return np.exp2(np.random.permutation(np.resize(levels, k // 32))).repeat(32)
    a = np.empty((k // 512, 16))
    for p in range(k // 512):
        a[p, :8] = np.random.permutation(np.resize(levels, 8))
        for g in range(8):
            far = levels[np.abs(levels - a[p, g]) >= 10]
            a[p, g + 8] = far[np.random.randint(len(far))]
    return np.exp2(a.ravel()).repeat(32)


def f64(x):
    return np.asarray(x).astype(np.float64)


def striped(idx):
    return np.tile(idx.reshape(-1, 16).T, (8, 1)).astype(np.uint16)


def unstriped(offs):
    return offs[:16].T.reshape(-1).astype(np.int64)


def pack_weight(w):
    k, n = w.shape
    w = f64(np.asarray(w, np.float32).astype(ml_dtypes.bfloat16)).reshape(k // 32, 32, n)
    amax = np.abs(w).max(1)
    byte = np.clip(np.where(amax > 0, np.frexp(amax)[1] - 1 + 127 - 7, 1), 1, 254)
    scaled = (w * np.exp2(127.0 - byte)[:, None, :]).reshape(k, n).astype(np.float32)
    words = np.ascontiguousarray(scaled.reshape(k // 512, 128, 4, n).transpose(0, 1, 3, 2)).astype(ml_dtypes.float8_e4m3fn).view(np.uint8)
    return words, np.ascontiguousarray(byte.astype(np.uint8).reshape(k // 512, 16, n))


def unpack_weight(words, scales):
    g, p, n, _ = words.shape
    vals = np.ascontiguousarray(words).view(ml_dtypes.float8_e4m3fn).astype(np.float64) * np.repeat(np.exp2(scales.astype(np.float64) - 127.0), 8, axis=1)[..., None]
    return vals.transpose(0, 1, 3, 2).reshape(g * 512, n)


def sigmoid(v):
    return 1.0 / (1.0 + np.exp(-np.maximum(v, -700.0)))


K, T, S, D, H, Z, W = 512, 2048, 512, 2, 512, 512, 2048
P = 2 ** 7


def setup_inputs():
    n = np.random.standard_normal
    s = mx_kscale(K)[:, None]
    packed_xT = pack_weight(n((K, T)) * s)
    packed_eT = pack_weight(n((K, W)) * s)
    return {
        "x_words": packed_xT[0],
        "x_scales": packed_xT[1],
        "w1": (n((K, H)) / np.sqrt(K) / s).astype(np.float32),
        "w2": (n((K, H)) / np.sqrt(K) / s).astype(np.float32),
        "e_words": packed_eT[0],
        "e_scales": packed_eT[1],
        "unit": (np.random.uniform(0.6, 1.4, (K, 1)) / np.sqrt(K) / s).astype(np.float32),
        "ndw": (np.tile(np.random.uniform(0.2, 1.2, W), (P, 1))).astype(np.float32),
        "offs": striped(np.random.permutation(T)[:S]),
        "qry": striped(np.random.permutation(W)[:Z]),
        "prtn": striped(np.random.permutation(Z)),
    }


def reference(x_words, x_scales, w1, w2, e_words, e_scales, unit, ndw, offs, qry, prtn):
    xq = unpack_weight(x_words, x_scales)[:, unstriped(offs)]
    y = mxq(f64(w1), 0, "e4m3").T @ xq
    yg = mxq(f64(w2), 0, "e4m3").T @ xq
    yw = y * sigmoid(yg)
    pass_ = yw.reshape(len(yw), -1, D).max(axis=2)
    p2 = (pass_) ** 2
    ms = p2.mean(axis=1, keepdims=True)
    np_ = pass_ / np.sqrt(ms + 0.1)
    hid = f64(unit) * np_
    e_qry = unpack_weight(e_words, e_scales)[:, unstriped(qry)]
    sc = mxq(hid, 0, "e4m3").T @ e_qry
    spar = sc[:, unstriped(prtn)]
    gap = sc - spar
    return gap * (f64(ndw)[:1][:, unstriped(qry)]) - (0.3 * ((spar) ** 2))

@@ -1,0 +1,197 @@
+import math
+from contextlib import ExitStack
+
+import concourse.mybir as mybir
+
+F32 = mybir.dt.float32
+BF16 = mybir.dt.bfloat16
+I32 = mybir.dt.int32
+U32 = mybir.dt.uint32
+U16 = mybir.dt.uint16
+U8 = mybir.dt.uint8
+FP8X4 = mybir.dt.float8_e4m3fn_x4
+ALU = mybir.AluOpType
+ACT = mybir.ActivationFunctionType
+
+P = 128
+PACK = 4
+K, T, S, H, Z, V = 512, 2048, 512, 512, 512, 256
+EPS = 0.1
+PENALTY = 0.3
+FLOPS = 2 * K * H * S * 2 + 2 * H * V * Z
+
+
+def tile_picked_yrerank_gap_p_kernel(
+    tc, x_words, x_scales, w1, w2, e_words, e_scales, unit, ndw, offs, qry, prtn, out
+):
+    nc = tc.nc
+    with ExitStack() as ctx:
+        pool = ctx.enter_context(tc.tile_pool(name="sb", bufs=1))
+        psum = ctx.enter_context(tc.psum_pool(name="ps", bufs=1))
+
+        def sb(name, shape, dtype):
+            return pool.tile(shape, dtype, name=name, align_bytes=64)
+
+        offs_t = sb("offs_t", [P, S // 16], U16)
+        qry_t = sb("qry_t", [P, Z // 16], U16)
+        prtn_t = sb("prtn_t", [P, Z // 16], U16)
+        x_tab = sb("x_tab", [P, T], U32)
+        e_tab = sb("e_tab", [P, T], U32)
+        x_stab = sb("x_stab", [P, T], U8)
+        e_stab = sb("e_stab", [P, T], U8)
+        ndw_tab = sb("ndw_tab", [P, T], F32)
+        unit_t = sb("unit_t", [P, PACK], F32)
+
+        nc.vector.memset(x_stab[:].bitcast(I32), 0)
+        nc.vector.memset(e_stab[:].bitcast(I32), 0)
+
+        def load_scales(tab, scales):
+            for q in range(4):
+                nc.scalar.dma_start(tab[32 * q : 32 * q + 4, :].bitcast(I32), scales[0][4 * q : 4 * q + 4, :].bitcast(I32))
+
+        def load_words(tab, words):
+            nc.sync.dma_start(tab[:].bitcast(I32), words[0].rearrange("p n t -> p (n t)").bitcast(I32))
+
+        def load_w(name, w):
+            halves = []
+            for h in range(2):
+                raw = sb("%s_raw%d" % (name, h), [P, PACK, H // 2], F32)
+                nc.sync.dma_start(raw[:], w[:, h * (H // 2) : (h + 1) * (H // 2)].rearrange("(p j) c -> p j c", j=PACK))
+                halves.append(raw)
+            return halves
+
+        load_words(x_tab, x_words)
+        nc.sync.dma_start(offs_t[:], offs)
+        load_scales(x_stab, x_scales)
+        w2_raw = load_w("w2", w2)
+        nc.sync.dma_start(qry_t[:], qry)
+        load_scales(e_stab, e_scales)
+        w1_raw = load_w("w1", w1)
+        nc.sync.dma_start(unit_t[:], unit.rearrange("(p t) o -> p (t o)", t=PACK))
+        nc.sync.dma_start(prtn_t[:], prtn)
+        load_words(e_tab, e_words)
+        nc.sync.dma_start(ndw_tab[:], ndw)
+
+        PADW = V + 8
+        kept = sb("kept", [P, PACK, PADW], F32)
+        nc.vector.memset(kept[:, :, V : V + 1], 1.0)
+        nc.vector.tensor_scalar(kept[:, :, V : V + 1], kept[:, :, V : V + 1], math.sqrt(EPS * V), None, ALU.mult)
+        minus_half = sb("minus_half", [P, 1], F32)
+        nc.gpsimd.memset(minus_half[:], -0.5)
+
+        x_s = sb("x_s", [P, S], U8)
+        x_c = sb("x_c", [P, S], U32)
+        e_s = sb("e_s", [P, Z], U8)
+        e_c = sb("e_c", [P, Z], U32)
+        nc.vector.tensor_copy(x_s[:], x_stab[:].indirect(offs_t[:]))
+        nc.vector.tensor_copy(x_c[:], x_tab[:].indirect(offs_t[:]))
+        nc.vector.tensor_copy(e_s[:], e_stab[:].indirect(qry_t[:]))
+
+        def weave(dst, raw, m0, c0, c1, on_scalar):
+            src = raw[:, :, c0:c1].rearrange("p j (m t) -> p m j t", t=PACK)
+            n = (c1 - c0) // PACK
+            o = dst[:, :, m0 : m0 + n, :].rearrange("p t m j -> p m j t")
+            if on_scalar:
+                nc.scalar.copy(o, src)
+            else:
+                nc.vector.tensor_copy(o, src)
+
+        def quant(name, woven, t):
+            codes = sb("%s_c%d" % (name, t), [P, P], U32)
+            scales = sb("%s_s%d" % (name, t), [P, P], U8)
+            nc.vector.quantize_mx(codes[:].bitcast(FP8X4), scales[:], woven[:, t, :, :].rearrange("p m j -> p (m j)"))
+            return codes, scales
+
+        w2_woven = sb("w2_woven", [P, PACK, P, PACK], BF16)
+        weave(w2_woven, w2_raw[0], 0, 0, 256, True)
+        weave(w2_woven, w2_raw[1], 64, 0, 256, False)
+        gates = []
+        for t in range(PACK):
+            codes, scales = quant("w2", w2_woven, t)
+            bank = psum.tile([P, S], F32, name="g%d" % t, tag="g%d" % t)
+            nc.tensor.matmul_mx(bank[:], codes[:].bitcast(FP8X4), scales[:], x_c[:].bitcast(FP8X4), x_s[:], start=True, stop=True)
+            gate = sb("gate%d" % t, [P, S], F32)
+            nc.scalar.activation(gate[:], bank[:], ACT.Sigmoid)
+            gates.append(gate)
+
+        w1_woven = sb("w1_woven", [P, PACK, P, PACK], BF16)
+        weave(w1_woven, w1_raw[0], 0, 0, 256, False)
+        weave(w1_woven, w1_raw[1], 64, 0, 256, False)
+        banks = []
+        for t in range(PACK):
+            codes, scales = quant("w1", w1_woven, t)
+            bank = psum.tile([P, S], F32, name="y%d" % t, tag="y%d" % t)
+            nc.tensor.matmul_mx(bank[:], codes[:].bitcast(FP8X4), scales[:], x_c[:].bitcast(FP8X4), x_s[:], start=True, stop=True)
+            banks.append(bank)
+
+        hid = sb("hid", [P, PACK, V], BF16)
+        gated = [sb("gated%d" % t, [P, V, 2], F32) for t in range(PACK)]
+
+        def gate_mult(t):
+            nc.vector.tensor_tensor(gated[t][:].rearrange("p v d -> p (v d)"), banks[t][:], gates[t][:], ALU.mult)
+
+        def keep_and_norm(t):
+            nc.vector.tensor_tensor(kept[:, t, :V], gated[t][:, :, 0], gated[t][:, :, 1], ALU.max)
+            sq = sb("sq%d" % t, [P, V + 1], F32)
+            ms = sb("ms%d" % t, [P, 1], F32)
+            nc.scalar.activation(sq[:], kept[:, t, : V + 1], ACT.Square, scale=1.0 / math.sqrt(V), accum_out=ms[:])
+            rstd = sb("rstd%d" % t, [P, 1], F32)
+            nc.gpsimd.tensor_tensor(rstd[:], ms[:], minus_half[:], ALU.pow)
+            fac = sb("fac%d" % t, [P, 1], F32)
+            nc.gpsimd.tensor_tensor(fac[:], rstd[:], unit_t[:, t : t + 1], ALU.mult)
+            nc.scalar.activation(hid[:, t, :], kept[:, t, :V], ACT.Copy, scale=fac[:])
+
+        gate_mult(0)
+        for t in range(1, PACK):
+            gate_mult(t)
+            keep_and_norm(t - 1)
+        keep_and_norm(PACK - 1)
+
+        nc.vector.tensor_copy(e_c[:], e_tab[:].indirect(qry_t[:]))
+        wq = sb("wq", [P, Z], F32)
+        nc.scalar.activation(wq[:], ndw_tab[:].indirect(qry_t[:]), ACT.Copy)
+
+        NB = V // P
+        HZ = Z // 2
+        woven = []
+        for b in range(NB):
+            hw = sb("hid_woven%d" % b, [P, P, PACK], BF16)
+            nc.vector.tensor_copy(
+                hw[:].rearrange("p (c i) t -> p c t i", i=4),
+                hid[:, :, b * P : (b + 1) * P].rearrange("p t (c i) -> p c t i", i=4),
+            )
+            woven.append(hw)
+        scs = []
+        for b in range(NB):
+            codes = sb("h_c%d" % b, [P, P], U32)
+            scales = sb("h_s%d" % b, [P, P], U8)
+            nc.vector.quantize_mx(codes[:].bitcast(FP8X4), scales[:], woven[b][:].rearrange("p v t -> p (v t)"))
+            sc = sb("sc%d" % b, [P, Z], F32)
+            for h in range(2):
+                cols = slice(h * HZ, (h + 1) * HZ)
+                bank = psum.tile([P, HZ], F32, name="s%d%d" % (b, h), tag="g%d" % (2 * b + h))
+                nc.tensor.matmul_mx(bank[:], codes[:].bitcast(FP8X4), scales[:], e_c[:, cols].bitcast(FP8X4), e_s[:, cols], start=True, stop=True)
+                if h == 1 and b == 0:
+                    nc.vector.tensor_copy(sc[:, cols], bank[:])
+                else:
+                    nc.scalar.copy(sc[:, cols], bank[:])
+            scs.append(sc)
+
+        for b in range(NB):
+            for h in range(2):
+                cols = slice(h * HZ, (h + 1) * HZ)
+                lst = prtn_t[:, h * (HZ // 16) : (h + 1) * (HZ // 16)]
+                spar = sb("spar%d%d" % (b, h), [P, HZ], F32)
+                if b == 0 and h == 1:
+                    nc.vector.tensor_copy(spar[:], scs[b][:].indirect(lst))
+                else:
+                    nc.scalar.activation(spar[:], scs[b][:].indirect(lst), ACT.Copy)
+                pen = sb("pen%d%d" % (b, h), [P, HZ], F32)
+                nc.scalar.activation(pen[:], spar[:], ACT.Square, scale=math.sqrt(PENALTY))
+                gap = sb("gap%d%d" % (b, h), [P, HZ], F32)
+                nc.vector.tensor_tensor(gap[:], scs[b][:, cols], spar[:], ALU.subtract)
+                wgap = sb("wgap%d%d" % (b, h), [P, HZ], F32)
+                nc.vector.tensor_tensor(wgap[:], gap[:], wq[:, cols], ALU.mult)
+                res = sb("res%d%d" % (b, h), [P, HZ], F32)
+                nc.vector.tensor_tensor(res[:], wgap[:], pen[:], ALU.subtract)
+                nc.sync.dma_start(out[b * P : (b + 1) * P, cols], res[:])

@@ -29,8 +29,8 @@ def tile_picked_yrerank_gap_p_kernel(
         pool = ctx.enter_context(tc.tile_pool(name="sb", bufs=1))
         psum = ctx.enter_context(tc.psum_pool(name="ps", bufs=1))
 
-        def sb(name, shape, dtype):
-            return pool.tile(shape, dtype, name=name, align_bytes=64)
+        def sb(name, shape, dtype, tag=None):
+            return pool.tile(shape, dtype, name=name, tag=tag or name, align_bytes=64)
 
         offs_t = sb("offs_t", [P, S // 16], U16)
         qry_t = sb("qry_t", [P, Z // 16], U16)
@@ -42,35 +42,34 @@ def tile_picked_yrerank_gap_p_kernel(
         ndw_tab = sb("ndw_tab", [P, T], F32)
         unit_t = sb("unit_t", [P, PACK], F32)
 
-        nc.vector.memset(x_stab[:].bitcast(I32), 0)
-        nc.vector.memset(e_stab[:].bitcast(I32), 0)
 
-        def load_scales(tab, scales):
+        nc.gpsimd.memset(e_stab[:].bitcast(I32), 0)
+        for q in range(4):
+            nc.gpsimd.dma_start(e_stab[32 * q : 32 * q + 4, :].bitcast(I32), e_scales[0][4 * q : 4 * q + 4, :].bitcast(I32))
+
+        def load_scales(queue, tab, scales):
             for q in range(4):
-                nc.scalar.dma_start(tab[32 * q : 32 * q + 4, :].bitcast(I32), scales[0][4 * q : 4 * q + 4, :].bitcast(I32))
+                queue.dma_start(tab[32 * q : 32 * q + 32, :].bitcast(I32), scales[0][4 * q : 4 * q + 4, :].bitcast(I32).partition_broadcast(8))
 
         def load_words(tab, words):
             nc.sync.dma_start(tab[:].bitcast(I32), words[0].rearrange("p n t -> p (n t)").bitcast(I32))
 
-        def load_w(name, w):
-            halves = []
-            for h in range(2):
-                raw = sb("%s_raw%d" % (name, h), [P, PACK, H // 2], F32)
-                nc.sync.dma_start(raw[:], w[:, h * (H // 2) : (h + 1) * (H // 2)].rearrange("(p j) c -> p j c", j=PACK))
-                halves.append(raw)
-            return halves
+        def load_w(name, w, h):
+            c0, c1 = h
+            raw = sb("%s_raw%d" % (name, c0), [P, PACK, c1 - c0], F32)
+            nc.sync.dma_start(raw[:], w[:, c0:c1].rearrange("(p j) c -> p j c", j=PACK))
+            return raw
 
-        load_words(x_tab, x_words)
         nc.sync.dma_start(offs_t[:], offs)
-        load_scales(x_stab, x_scales)
-        w2_raw = load_w("w2", w2)
         nc.sync.dma_start(qry_t[:], qry)
-        load_scales(e_stab, e_scales)
-        w1_raw = load_w("w1", w1)
-        nc.sync.dma_start(unit_t[:], unit.rearrange("(p t) o -> p (t o)", t=PACK))
+        w2_raw = [load_w("w2", w2, h) for h in ((0, 256), (256, 512))]
+        load_scales(nc.sync, x_stab, x_scales)
+        load_words(x_tab, x_words)
+        w1_raw = [load_w("w1", w1, h) for h in ((0, 384), (384, 512))]
         nc.sync.dma_start(prtn_t[:], prtn)
         load_words(e_tab, e_words)
         nc.sync.dma_start(ndw_tab[:], ndw)
+        nc.sync.dma_start(unit_t[:], unit.rearrange("(p t) o -> p (t o)", t=PACK))
 
         PADW = V + 8
         kept = sb("kept", [P, PACK, PADW], F32)
@@ -81,10 +80,10 @@ def tile_picked_yrerank_gap_p_kernel(
 
         x_s = sb("x_s", [P, S], U8)
         x_c = sb("x_c", [P, S], U32)
-        e_s = sb("e_s", [P, Z], U8)
-        e_c = sb("e_c", [P, Z], U32)
         nc.vector.tensor_copy(x_s[:], x_stab[:].indirect(offs_t[:]))
         nc.vector.tensor_copy(x_c[:], x_tab[:].indirect(offs_t[:]))
+
+        e_s = sb("e_s", [P, Z], U8, tag="x_tab")
         nc.vector.tensor_copy(e_s[:], e_stab[:].indirect(qry_t[:]))
 
         def weave(dst, raw, m0, c0, c1, on_scalar):
@@ -115,8 +114,8 @@ def tile_picked_yrerank_gap_p_kernel(
             gates.append(gate)
 
         w1_woven = sb("w1_woven", [P, PACK, P, PACK], BF16)
-        weave(w1_woven, w1_raw[0], 0, 0, 256, False)
-        weave(w1_woven, w1_raw[1], 64, 0, 256, False)
+        weave(w1_woven, w1_raw[0], 0, 0, 384, False)
+        weave(w1_woven, w1_raw[1], 96, 0, 128, False)
         banks = []
         for t in range(PACK):
             codes, scales = quant("w1", w1_woven, t)
@@ -132,14 +131,17 @@ def tile_picked_yrerank_gap_p_kernel(
 
         def keep_and_norm(t):
             nc.vector.tensor_tensor(kept[:, t, :V], gated[t][:, :, 0], gated[t][:, :, 1], ALU.max)
-            sq = sb("sq%d" % t, [P, V + 1], F32)
+            sq = sb("sq%d" % t, [P, V + 1], F32, tag="sq")
             ms = sb("ms%d" % t, [P, 1], F32)
             nc.scalar.activation(sq[:], kept[:, t, : V + 1], ACT.Square, scale=1.0 / math.sqrt(V), accum_out=ms[:])
             rstd = sb("rstd%d" % t, [P, 1], F32)
             nc.gpsimd.tensor_tensor(rstd[:], ms[:], minus_half[:], ALU.pow)
-            fac = sb("fac%d" % t, [P, 1], F32)
-            nc.gpsimd.tensor_tensor(fac[:], rstd[:], unit_t[:, t : t + 1], ALU.mult)
-            nc.scalar.activation(hid[:, t, :], kept[:, t, :V], ACT.Copy, scale=fac[:])
+            if t >= PACK - 2:
+                nc.vector.tensor_scalar(hid[:, t, :], kept[:, t, :V], rstd[:], unit_t[:, t : t + 1], ALU.mult, ALU.mult)
+            else:
+                scaled = sb("scaled%d" % t, [P, V], F32)
+                nc.scalar.activation(scaled[:], kept[:, t, :V], ACT.Copy, scale=unit_t[:, t : t + 1])
+                nc.scalar.activation(hid[:, t, :], scaled[:], ACT.Copy, scale=rstd[:])
 
         gate_mult(0)
         for t in range(1, PACK):
@@ -147,8 +149,9 @@ def tile_picked_yrerank_gap_p_kernel(
             keep_and_norm(t - 1)
         keep_and_norm(PACK - 1)
 
+        e_c = sb("e_c", [P, Z], U32, tag="gated%d" % (PACK - 1))
         nc.vector.tensor_copy(e_c[:], e_tab[:].indirect(qry_t[:]))
-        wq = sb("wq", [P, Z], F32)
+        wq = sb("wq", [P, Z], F32, tag="scaled1")
         nc.scalar.activation(wq[:], ndw_tab[:].indirect(qry_t[:]), ACT.Copy)
 
         NB = V // P
@@ -161,37 +164,71 @@ def tile_picked_yrerank_gap_p_kernel(
                 hid[:, :, b * P : (b + 1) * P].rearrange("p t (c i) -> p c t i", i=4),
             )
             woven.append(hw)
-        scs = []
+        banks = {}
         for b in range(NB):
             codes = sb("h_c%d" % b, [P, P], U32)
             scales = sb("h_s%d" % b, [P, P], U8)
             nc.vector.quantize_mx(codes[:].bitcast(FP8X4), scales[:], woven[b][:].rearrange("p v t -> p (v t)"))
-            sc = sb("sc%d" % b, [P, Z], F32)
             for h in range(2):
                 cols = slice(h * HZ, (h + 1) * HZ)
                 bank = psum.tile([P, HZ], F32, name="s%d%d" % (b, h), tag="g%d" % (2 * b + h))
                 nc.tensor.matmul_mx(bank[:], codes[:].bitcast(FP8X4), scales[:], e_c[:, cols].bitcast(FP8X4), e_s[:, cols], start=True, stop=True)
-                if h == 1 and b == 0:
-                    nc.vector.tensor_copy(sc[:, cols], bank[:])
-                else:
-                    nc.scalar.copy(sc[:, cols], bank[:])
-            scs.append(sc)
+                banks[b, h] = bank
 
-        for b in range(NB):
-            for h in range(2):
-                cols = slice(h * HZ, (h + 1) * HZ)
-                lst = prtn_t[:, h * (HZ // 16) : (h + 1) * (HZ // 16)]
-                spar = sb("spar%d%d" % (b, h), [P, HZ], F32)
-                if b == 0 and h == 1:
-                    nc.vector.tensor_copy(spar[:], scs[b][:].indirect(lst))
-                else:
-                    nc.scalar.activation(spar[:], scs[b][:].indirect(lst), ACT.Copy)
-                pen = sb("pen%d%d" % (b, h), [P, HZ], F32)
-                nc.scalar.activation(pen[:], spar[:], ACT.Square, scale=math.sqrt(PENALTY))
-                gap = sb("gap%d%d" % (b, h), [P, HZ], F32)
-                nc.vector.tensor_tensor(gap[:], scs[b][:, cols], spar[:], ALU.subtract)
-                wgap = sb("wgap%d%d" % (b, h), [P, HZ], F32)
-                nc.vector.tensor_tensor(wgap[:], gap[:], wq[:, cols], ALU.mult)
-                res = sb("res%d%d" % (b, h), [P, HZ], F32)
-                nc.vector.tensor_tensor(res[:], wgap[:], pen[:], ALU.subtract)
-                nc.sync.dma_start(out[b * P : (b + 1) * P, cols], res[:])
+        scs = [sb("sc%d" % b, [P, Z], F32) for b in range(NB)]
+        names = ("spar", "pen", "gap", "wgap", "res")
+        tl = {(n, b, h): sb("%s%d%d" % (n, b, h), [P, HZ], F32) for n in names for b in range(NB) for h in range(2)}
+
+        def half(h):
+            return slice(h * HZ, (h + 1) * HZ)
+
+        def drain(b, h, on_vector):
+            if on_vector:
+                nc.vector.tensor_copy(scs[b][:, half(h)], banks[b, h][:])
+            else:
+                nc.scalar.copy(scs[b][:, half(h)], banks[b, h][:])
+
+        def fetch(b, h, on_vector):
+            src = scs[b][:].indirect(prtn_t[:, h * (HZ // 16) : (h + 1) * (HZ // 16)])
+            if on_vector:
+                nc.vector.tensor_copy(tl["spar", b, h][:], src)
+            else:
+                nc.scalar.activation(tl["spar", b, h][:], src, ACT.Copy)
+
+        def square(b, h):
+            nc.scalar.activation(tl["pen", b, h][:], tl["spar", b, h][:], ACT.Square, scale=math.sqrt(PENALTY))
+
+        def weigh(b, h):
+            nc.vector.tensor_tensor(tl["gap", b, h][:], scs[b][:, half(h)], tl["spar", b, h][:], ALU.subtract)
+
+        def weigh2(b, h):
+            nc.vector.tensor_tensor(tl["wgap", b, h][:], tl["gap", b, h][:], wq[:, half(h)], ALU.mult)
+
+        def finish(b, h):
+            nc.vector.tensor_tensor(tl["res", b, h][:], tl["wgap", b, h][:], tl["pen", b, h][:], ALU.subtract)
+            nc.sync.dma_start(out[b * P : (b + 1) * P, half(h)], tl["res", b, h][:])
+
+        drain(0, 0, False)
+        drain(0, 1, True)
+        fetch(0, 1, True)
+        fetch(0, 0, False)
+        drain(1, 0, False)
+        drain(1, 1, False)
+        fetch(1, 1, False)
+        square(0, 1)
+        fetch(1, 0, False)
+        square(0, 0)
+        square(1, 1)
+        square(1, 0)
+        weigh(0, 1)
+        weigh(0, 0)
+        weigh2(0, 1)
+        weigh2(0, 0)
+        weigh(1, 1)
+        finish(0, 1)
+        weigh2(1, 1)
+        weigh(1, 0)
+        finish(0, 0)
+        weigh2(1, 0)
+        finish(1, 1)
+        finish(1, 0)

@@ -36,55 +36,48 @@ def tile_picked_yrerank_gap_p_kernel(
         qry_t = sb("qry_t", [P, Z // 16], U16)
         prtn_t = sb("prtn_t", [P, Z // 16], U16)
         x_tab = sb("x_tab", [P, T], U32)
-        e_tab = sb("e_tab", [P, T], U32)
         x_stab = sb("x_stab", [P, T], U8)
         e_stab = sb("e_stab", [P, T], U8)
-        ndw_tab = sb("ndw_tab", [P, T], F32)
         unit_t = sb("unit_t", [P, PACK], F32)
-
-
-        nc.gpsimd.memset(e_stab[:].bitcast(I32), 0)
-        for q in range(4):
-            nc.gpsimd.dma_start(e_stab[32 * q : 32 * q + 4, :].bitcast(I32), e_scales[0][4 * q : 4 * q + 4, :].bitcast(I32))
-
-        def load_scales(queue, tab, scales):
-            for q in range(4):
-                queue.dma_start(tab[32 * q : 32 * q + 32, :].bitcast(I32), scales[0][4 * q : 4 * q + 4, :].bitcast(I32).partition_broadcast(8))
 
         def load_words(tab, words):
             nc.sync.dma_start(tab[:].bitcast(I32), words[0].rearrange("p n t -> p (n t)").bitcast(I32))
 
-        def load_w(name, w, h):
-            c0, c1 = h
-            raw = sb("%s_raw%d" % (name, c0), [P, PACK, c1 - c0], F32)
+        def load_w(name, w, c0, c1, tag):
+            raw = sb("%s_raw%d" % (name, c0), [P, PACK, c1 - c0], F32, tag=tag)
             nc.sync.dma_start(raw[:], w[:, c0:c1].rearrange("(p j) c -> p j c", j=PACK))
             return raw
 
+        nc.gpsimd.memset(e_stab[:].bitcast(I32), 0)
+        nc.gpsimd.dma_start(unit_t[:], unit.rearrange("(p t) o -> p (t o)", t=PACK))
         nc.sync.dma_start(offs_t[:], offs)
         nc.sync.dma_start(qry_t[:], qry)
-        w2_raw = [load_w("w2", w2, h) for h in ((0, 256), (256, 512))]
-        load_scales(nc.sync, x_stab, x_scales)
+        w2_raw = [load_w("w2", w2, 0, 256, "raw0"), load_w("w2", w2, 256, 512, "raw1")]
+        for q in range(4):
+            nc.sync.dma_start(x_stab[32 * q : 32 * q + 32, :].bitcast(I32), x_scales[0][4 * q : 4 * q + 4, :].bitcast(I32).partition_broadcast(8))
         load_words(x_tab, x_words)
-        w1_raw = [load_w("w1", w1, h) for h in ((0, 384), (384, 512))]
         nc.sync.dma_start(prtn_t[:], prtn)
-        load_words(e_tab, e_words)
-        nc.sync.dma_start(ndw_tab[:], ndw)
-        nc.sync.dma_start(unit_t[:], unit.rearrange("(p t) o -> p (t o)", t=PACK))
-
-        PADW = V + 8
-        kept = sb("kept", [P, PACK, PADW], F32)
-        nc.vector.memset(kept[:, :, V : V + 1], 1.0)
-        nc.vector.tensor_scalar(kept[:, :, V : V + 1], kept[:, :, V : V + 1], math.sqrt(EPS * V), None, ALU.mult)
-        minus_half = sb("minus_half", [P, 1], F32)
-        nc.gpsimd.memset(minus_half[:], -0.5)
+        for q in range(4):
+            nc.sync.dma_start(e_stab[32 * q : 32 * q + 4, :].bitcast(I32), e_scales[0][4 * q : 4 * q + 4, :].bitcast(I32))
 
         x_s = sb("x_s", [P, S], U8)
-        x_c = sb("x_c", [P, S], U32)
+        x_c = [sb("x_c%d" % h, [P, S // 2], U32) for h in range(2)]
         nc.vector.tensor_copy(x_s[:], x_stab[:].indirect(offs_t[:]))
-        nc.vector.tensor_copy(x_c[:], x_tab[:].indirect(offs_t[:]))
+        for h in range(2):
+            nc.vector.tensor_copy(x_c[h][:], x_tab[:].indirect(offs_t[:, 16 * h : 16 * (h + 1)]))
+        e_s = []
 
-        e_s = sb("e_s", [P, Z], U8, tag="x_tab")
-        nc.vector.tensor_copy(e_s[:], e_stab[:].indirect(qry_t[:]))
+        def gather_e_scales(h, tag):
+            part = sb("e_s%d" % h, [P, Z // 2], U8, tag=tag)
+            nc.vector.tensor_copy(part[:], e_stab[:].indirect(qry_t[:, 16 * h : 16 * (h + 1)]))
+            e_s.append(part)
+
+        gather_e_scales(0, "x_tab")
+
+        def product(bank, codes, scales):
+            for h in range(2):
+                cols = slice(256 * h, 256 * (h + 1))
+                nc.tensor.matmul_mx(bank[:, cols], codes.bitcast(FP8X4), scales, x_c[h][:].bitcast(FP8X4), x_s[:, cols], start=True, stop=True)
 
         def weave(dst, raw, m0, c0, c1, on_scalar):
             src = raw[:, :, c0:c1].rearrange("p j (m t) -> p m j t", t=PACK)
@@ -95,63 +88,83 @@ def tile_picked_yrerank_gap_p_kernel(
             else:
                 nc.vector.tensor_copy(o, src)
 
-        def quant(name, woven, t):
-            codes = sb("%s_c%d" % (name, t), [P, P], U32)
-            scales = sb("%s_s%d" % (name, t), [P, P], U8)
-            nc.vector.quantize_mx(codes[:].bitcast(FP8X4), scales[:], woven[:, t, :, :].rearrange("p m j -> p (m j)"))
+        def quant(name, woven):
+            codes = sb(name + "_c", [P, PACK, P], U32)
+            scales = sb(name + "_s", [P, PACK, P], U8)
+            for t0, t1 in ((0, 1), (1, PACK)):
+                nc.vector.quantize_mx(
+                    codes[:, t0:t1, :].rearrange("p t m -> p (t m)").bitcast(FP8X4),
+                    scales[:, t0:t1, :].rearrange("p t m -> p (t m)"),
+                    woven[:, t0:t1, :, :].rearrange("p t m j -> p (t m j)"),
+                )
             return codes, scales
 
         w2_woven = sb("w2_woven", [P, PACK, P, PACK], BF16)
         weave(w2_woven, w2_raw[0], 0, 0, 256, True)
         weave(w2_woven, w2_raw[1], 64, 0, 256, False)
+        w1_raw = [load_w("w1", w1, 0, 320, "raw0"), load_w("w1", w1, 320, 512, "raw1")]
+        e_tab = sb("e_tab", [P, T], U32, tag="x_stab")
+        load_words(e_tab, e_words)
         gates = []
+        codes, scales = quant("w2", w2_woven)
         for t in range(PACK):
-            codes, scales = quant("w2", w2_woven, t)
             bank = psum.tile([P, S], F32, name="g%d" % t, tag="g%d" % t)
-            nc.tensor.matmul_mx(bank[:], codes[:].bitcast(FP8X4), scales[:], x_c[:].bitcast(FP8X4), x_s[:], start=True, stop=True)
+            product(bank, codes[:, t, :], scales[:, t, :])
             gate = sb("gate%d" % t, [P, S], F32)
             nc.scalar.activation(gate[:], bank[:], ACT.Sigmoid)
-            gates.append(gate)
+            gates.append(gate[:])
 
         w1_woven = sb("w1_woven", [P, PACK, P, PACK], BF16)
-        weave(w1_woven, w1_raw[0], 0, 0, 384, False)
-        weave(w1_woven, w1_raw[1], 96, 0, 128, False)
+        weave(w1_woven, w1_raw[0], 0, 0, 320, False)
+        weave(w1_woven, w1_raw[1], 80, 0, 192, False)
         banks = []
+        codes, scales = quant("w1", w1_woven)
         for t in range(PACK):
-            codes, scales = quant("w1", w1_woven, t)
             bank = psum.tile([P, S], F32, name="y%d" % t, tag="y%d" % t)
-            nc.tensor.matmul_mx(bank[:], codes[:].bitcast(FP8X4), scales[:], x_c[:].bitcast(FP8X4), x_s[:], start=True, stop=True)
+            product(bank, codes[:, t, :], scales[:, t, :])
             banks.append(bank)
 
+        gather_e_scales(1, "w1_woven")
+        ndw_tab = sb("ndw_tab", [P, T], F32, tag="raw0")
+        nc.sync.dma_start(ndw_tab[:], ndw)
+        kept = sb("kept", [P, PACK, V], F32)
         hid = sb("hid", [P, PACK, V], BF16)
         gated = [sb("gated%d" % t, [P, V, 2], F32) for t in range(PACK)]
 
         def gate_mult(t):
-            nc.vector.tensor_tensor(gated[t][:].rearrange("p v d -> p (v d)"), banks[t][:], gates[t][:], ALU.mult)
+            nc.vector.tensor_tensor(gated[t][:].rearrange("p v d -> p (v d)"), banks[t][:], gates[t], ALU.mult)
 
-        def keep_and_norm(t):
-            nc.vector.tensor_tensor(kept[:, t, :V], gated[t][:, :, 0], gated[t][:, :, 1], ALU.max)
-            sq = sb("sq%d" % t, [P, V + 1], F32, tag="sq")
-            ms = sb("ms%d" % t, [P, 1], F32)
-            nc.scalar.activation(sq[:], kept[:, t, : V + 1], ACT.Square, scale=1.0 / math.sqrt(V), accum_out=ms[:])
-            rstd = sb("rstd%d" % t, [P, 1], F32)
-            nc.gpsimd.tensor_tensor(rstd[:], ms[:], minus_half[:], ALU.pow)
-            if t >= PACK - 2:
-                nc.vector.tensor_scalar(hid[:, t, :], kept[:, t, :V], rstd[:], unit_t[:, t : t + 1], ALU.mult, ALU.mult)
-            else:
-                scaled = sb("scaled%d" % t, [P, V], F32)
-                nc.scalar.activation(scaled[:], kept[:, t, :V], ACT.Copy, scale=unit_t[:, t : t + 1])
-                nc.scalar.activation(hid[:, t, :], scaled[:], ACT.Copy, scale=rstd[:])
+        ss = [sb("ss%d" % u, [P, 2], F32) for u in range(2)]
+        rstd = [sb("rstd%d" % u, [P, 2], F32) for u in range(2)]
+
+        def keep(t):
+            nc.vector.tensor_tensor(kept[:, t, :], gated[t][:, :, 0], gated[t][:, :, 1], ALU.max)
+            sq = sb("sq%d" % t, [P, V], F32, tag="sq")
+            nc.scalar.activation(sq[:], kept[:, t, :], ACT.Square, accum_out=ss[t // 2][:, t % 2 : t % 2 + 1])
+
+        def inverse_root(u):
+            nc.scalar.activation(rstd[u][:], ss[u][:], ACT.Abs_reciprocal_sqrt, bias=EPS, scale=1.0 / V)
 
         gate_mult(0)
-        for t in range(1, PACK):
-            gate_mult(t)
-            keep_and_norm(t - 1)
-        keep_and_norm(PACK - 1)
+        gate_mult(1)
+        keep(0)
+        gate_mult(2)
+        keep(1)
+        inverse_root(0)
+        fac = sb("fac", [P, 2], F32)
+        nc.gpsimd.tensor_tensor(fac[:], rstd[0][:], unit_t[:, 0:2], ALU.mult)
+        gate_mult(3)
+        keep(2)
+        keep(3)
+        inverse_root(1)
+        for t in range(2):
+            nc.scalar.activation(hid[:, t, :], kept[:, t, :], ACT.Copy, scale=fac[:, t : t + 1])
 
         e_c = sb("e_c", [P, Z], U32, tag="gated%d" % (PACK - 1))
         nc.vector.tensor_copy(e_c[:], e_tab[:].indirect(qry_t[:]))
-        wq = sb("wq", [P, Z], F32, tag="scaled1")
+        for t in range(2, PACK):
+            nc.vector.tensor_scalar(hid[:, t, :], kept[:, t, :], rstd[1][:, t - 2 : t - 1], unit_t[:, t : t + 1], ALU.mult, ALU.mult)
+        wq = sb("wq", [P, Z], F32, tag="fac")
         nc.scalar.activation(wq[:], ndw_tab[:].indirect(qry_t[:]), ACT.Copy)
 
         NB = V // P
@@ -172,7 +185,7 @@ def tile_picked_yrerank_gap_p_kernel(
             for h in range(2):
                 cols = slice(h * HZ, (h + 1) * HZ)
                 bank = psum.tile([P, HZ], F32, name="s%d%d" % (b, h), tag="g%d" % (2 * b + h))
-                nc.tensor.matmul_mx(bank[:], codes[:].bitcast(FP8X4), scales[:], e_c[:, cols].bitcast(FP8X4), e_s[:, cols], start=True, stop=True)
+                nc.tensor.matmul_mx(bank[:], codes[:].bitcast(FP8X4), scales[:], e_c[:, cols].bitcast(FP8X4), e_s[h][:], start=True, stop=True)
                 banks[b, h] = bank
 
         scs = [sb("sc%d" % b, [P, Z], F32) for b in range(NB)]

@@ -35,58 +35,33 @@ def tile_picked_yrerank_gap_p_kernel(
         offs_t = sb("offs_t", [P, S // 16], U16)
         qry_t = sb("qry_t", [P, Z // 16], U16)
         prtn_t = sb("prtn_t", [P, Z // 16], U16)
-        x_tab = sb("x_tab", [P, T], U32)
-        x_stab = sb("x_stab", [P, T], U8)
-        e_stab = sb("e_stab", [P, T], U8)
         unit_t = sb("unit_t", [P, PACK], F32)
 
-        def load_words(tab, words):
+        def load_words(name, words, tag):
+            tab = sb(name, [P, T], U32, tag=tag)
             nc.sync.dma_start(tab[:].bitcast(I32), words[0].rearrange("p n t -> p (n t)").bitcast(I32))
+            return tab
+
+        def load_scales(name, scales, engine, tag):
+            tab = sb(name, [P, T], U8, tag=tag)
+            engine.memset(tab[:].bitcast(I32), 0)
+            for q in range(4):
+                nc.sync.dma_start(tab[32 * q : 32 * q + 4, :].bitcast(I32), scales[0][4 * q : 4 * q + 4, :].bitcast(I32))
+            return tab
 
         def load_w(name, w, c0, c1, tag):
             raw = sb("%s_raw%d" % (name, c0), [P, PACK, c1 - c0], F32, tag=tag)
             nc.sync.dma_start(raw[:], w[:, c0:c1].rearrange("(p j) c -> p j c", j=PACK))
             return raw
 
-        nc.gpsimd.memset(e_stab[:].bitcast(I32), 0)
-        nc.gpsimd.dma_start(unit_t[:], unit.rearrange("(p t) o -> p (t o)", t=PACK))
-        nc.sync.dma_start(offs_t[:], offs)
-        nc.sync.dma_start(qry_t[:], qry)
-        w2_raw = [load_w("w2", w2, 0, 256, "raw0"), load_w("w2", w2, 256, 512, "raw1")]
-        for q in range(4):
-            nc.sync.dma_start(x_stab[32 * q : 32 * q + 32, :].bitcast(I32), x_scales[0][4 * q : 4 * q + 4, :].bitcast(I32).partition_broadcast(8))
-        load_words(x_tab, x_words)
-        nc.sync.dma_start(prtn_t[:], prtn)
-        for q in range(4):
-            nc.sync.dma_start(e_stab[32 * q : 32 * q + 4, :].bitcast(I32), e_scales[0][4 * q : 4 * q + 4, :].bitcast(I32))
-
-        x_s = sb("x_s", [P, S], U8)
-        x_c = [sb("x_c%d" % h, [P, S // 2], U32) for h in range(2)]
-        nc.vector.tensor_copy(x_s[:], x_stab[:].indirect(offs_t[:]))
-        for h in range(2):
-            nc.vector.tensor_copy(x_c[h][:], x_tab[:].indirect(offs_t[:, 16 * h : 16 * (h + 1)]))
-        e_s = []
-
-        def gather_e_scales(h, tag):
-            part = sb("e_s%d" % h, [P, Z // 2], U8, tag=tag)
-            nc.vector.tensor_copy(part[:], e_stab[:].indirect(qry_t[:, 16 * h : 16 * (h + 1)]))
-            e_s.append(part)
-
-        gather_e_scales(0, "x_tab")
-
         def product(bank, codes, scales):
             for h in range(2):
                 cols = slice(256 * h, 256 * (h + 1))
                 nc.tensor.matmul_mx(bank[:, cols], codes.bitcast(FP8X4), scales, x_c[h][:].bitcast(FP8X4), x_s[:, cols], start=True, stop=True)
 
-        def weave(dst, raw, m0, c0, c1, on_scalar):
-            src = raw[:, :, c0:c1].rearrange("p j (m t) -> p m j t", t=PACK)
-            n = (c1 - c0) // PACK
-            o = dst[:, :, m0 : m0 + n, :].rearrange("p t m j -> p m j t")
-            if on_scalar:
-                nc.scalar.copy(o, src)
-            else:
-                nc.vector.tensor_copy(o, src)
+        def weave(dst, raw, c0, copy):
+            m0, n = c0 // PACK, raw.shape[2] // PACK
+            copy(dst[:, :, m0 : m0 + n, :].rearrange("p t m j -> p m j t"), raw[:].rearrange("p j (m t) -> p m j t", t=PACK))
 
         def quant(name, woven):
             codes = sb(name + "_c", [P, PACK, P], U32)
@@ -99,14 +74,45 @@ def tile_picked_yrerank_gap_p_kernel(
                 )
             return codes, scales
 
+        nc.gpsimd.dma_start(unit_t[:], unit.rearrange("(p t) o -> p (t o)", t=PACK))
+        w2_a = load_w("w2", w2, 0, 128, "slot_a")
+        nc.sync.dma_start(offs_t[:], offs)
+        nc.sync.dma_start(qry_t[:], qry)
+        nc.sync.dma_start(prtn_t[:], prtn)
+        w1_a = load_w("w1", w1, 0, 128, "slot_b")
+        w2_b = load_w("w2", w2, 128, 256, "slot_c")
+        w2_c = load_w("w2", w2, 256, 512, "slot_d")
+        x_stab = load_scales("x_stab", x_scales, nc.vector, None)
+
         w2_woven = sb("w2_woven", [P, PACK, P, PACK], BF16)
-        weave(w2_woven, w2_raw[0], 0, 0, 256, True)
-        weave(w2_woven, w2_raw[1], 64, 0, 256, False)
-        w1_raw = [load_w("w1", w1, 0, 320, "raw0"), load_w("w1", w1, 320, 512, "raw1")]
-        e_tab = sb("e_tab", [P, T], U32, tag="x_stab")
-        load_words(e_tab, e_words)
-        gates = []
+        w1_woven = sb("w1_woven", [P, PACK, P, PACK], BF16)
+        weave(w2_woven, w2_a, 0, nc.vector.tensor_copy)
+        x_tab = load_words("x_tab", x_words, "slot_a")
+        weave(w1_woven, w1_a, 0, nc.vector.tensor_copy)
+        e_stab = load_scales("e_stab", e_scales, nc.vector, "slot_b")
+        weave(w2_woven, w2_b, 128, nc.vector.tensor_copy)
+        w1_b = load_w("w1", w1, 128, 384, "slot_c")
+        weave(w2_woven, w2_c, 256, nc.scalar.copy)
+        w1_c = load_w("w1", w1, 384, 512, "slot_d")
+
+        x_s = sb("x_s", [P, S], U8)
+        x_c = [sb("x_c%d" % h, [P, S // 2], U32) for h in range(2)]
+        nc.vector.tensor_copy(x_s[:], x_stab[:].indirect(offs_t[:]))
         codes, scales = quant("w2", w2_woven)
+        e_tab = load_words("e_tab", e_words, "w2_woven")
+        for h in range(2):
+            nc.vector.tensor_copy(x_c[h][:], x_tab[:].indirect(offs_t[:, 16 * h : 16 * (h + 1)]))
+        ndw_tab = sb("ndw_tab", [P, T], F32, tag="slot_a")
+        nc.sync.dma_start(ndw_tab[:], ndw)
+        e_s = []
+
+        def gather_e_scales(h, tag):
+            part = sb("e_s%d" % h, [P, Z // 2], U8, tag=tag)
+            nc.vector.tensor_copy(part[:], e_stab[:].indirect(qry_t[:, 16 * h : 16 * (h + 1)]))
+            e_s.append(part)
+
+        gather_e_scales(0, None)
+        gates = []
         for t in range(PACK):
             bank = psum.tile([P, S], F32, name="g%d" % t, tag="g%d" % t)
             product(bank, codes[:, t, :], scales[:, t, :])
@@ -114,9 +120,10 @@ def tile_picked_yrerank_gap_p_kernel(
             nc.scalar.activation(gate[:], bank[:], ACT.Sigmoid)
             gates.append(gate[:])
 
-        w1_woven = sb("w1_woven", [P, PACK, P, PACK], BF16)
-        weave(w1_woven, w1_raw[0], 0, 0, 320, False)
-        weave(w1_woven, w1_raw[1], 80, 0, 192, False)
+        weave(w1_woven, w1_b, 128, nc.vector.tensor_copy)
+        weave(w1_woven, w1_c, 384, nc.vector.tensor_copy)
+        warm = sb("warm", [P, 1], F32)
+        nc.scalar.activation(warm[:], gates[PACK - 1][:, 0:1], ACT.Abs_reciprocal_sqrt, bias=EPS, scale=1.0 / V)
         banks = []
         codes, scales = quant("w1", w1_woven)
         for t in range(PACK):
@@ -125,8 +132,6 @@ def tile_picked_yrerank_gap_p_kernel(
             banks.append(bank)
 
         gather_e_scales(1, "w1_woven")
-        ndw_tab = sb("ndw_tab", [P, T], F32, tag="raw0")
-        nc.sync.dma_start(ndw_tab[:], ndw)
         kept = sb("kept", [P, PACK, V], F32)
         hid = sb("hid", [P, PACK, V], BF16)
         gated = [sb("gated%d" % t, [P, V, 2], F32) for t in range(PACK)]

import math
from contextlib import ExitStack

import concourse.mybir as mybir

F32 = mybir.dt.float32
BF16 = mybir.dt.bfloat16
I32 = mybir.dt.int32
U32 = mybir.dt.uint32
U16 = mybir.dt.uint16
U8 = mybir.dt.uint8
FP8X4 = mybir.dt.float8_e4m3fn_x4
ALU = mybir.AluOpType
ACT = mybir.ActivationFunctionType

P = 128
PACK = 4
K, T, S, H, Z, V = 512, 2048, 512, 512, 512, 256
EPS = 0.1
PENALTY = 0.3
FLOPS = 2 * K * H * S * 2 + 2 * H * V * Z


def tile_picked_yrerank_gap_p_kernel(
    tc, x_words, x_scales, w1, w2, e_words, e_scales, unit, ndw, offs, qry, prtn, out
):
    nc = tc.nc
    with ExitStack() as ctx:
        pool = ctx.enter_context(tc.tile_pool(name="sb", bufs=1))
        psum = ctx.enter_context(tc.psum_pool(name="ps", bufs=1))

        def sb(name, shape, dtype, tag=None):
            return pool.tile(shape, dtype, name=name, tag=tag or name, align_bytes=64)

        offs_t = sb("offs_t", [P, S // 16], U16)
        qry_t = sb("qry_t", [P, Z // 16], U16)
        prtn_t = sb("prtn_t", [P, Z // 16], U16)
        unit_t = sb("unit_t", [P, PACK], F32)

        def load_words(name, words, tag):
            tab = sb(name, [P, T], U32, tag=tag)
            nc.sync.dma_start(tab[:].bitcast(I32), words[0].rearrange("p n t -> p (n t)").bitcast(I32))
            return tab

        def load_scales(name, scales, engine, tag):
            tab = sb(name, [P, T], U8, tag=tag)
            engine.memset(tab[:].bitcast(I32), 0)
            for q in range(4):
                nc.sync.dma_start(tab[32 * q : 32 * q + 4, :].bitcast(I32), scales[0][4 * q : 4 * q + 4, :].bitcast(I32))
            return tab

        def load_w(name, w, c0, c1, tag):
            raw = sb("%s_raw%d" % (name, c0), [P, PACK, c1 - c0], F32, tag=tag)
            nc.sync.dma_start(raw[:], w[:, c0:c1].rearrange("(p j) c -> p j c", j=PACK))
            return raw

        def product(bank, codes, scales):
            for h in range(2):
                cols = slice(256 * h, 256 * (h + 1))
                nc.tensor.matmul_mx(bank[:, cols], codes.bitcast(FP8X4), scales, x_c[h][:].bitcast(FP8X4), x_s[:, cols], start=True, stop=True)

        def weave(dst, raw, c0, copy):
            m0, n = c0 // PACK, raw.shape[2] // PACK
            copy(dst[:, :, m0 : m0 + n, :].rearrange("p t m j -> p m j t"), raw[:].rearrange("p j (m t) -> p m j t", t=PACK))

        def quant(name, woven):
            codes = sb(name + "_c", [P, PACK, P], U32)
            scales = sb(name + "_s", [P, PACK, P], U8)
            for t0, t1 in ((0, 1), (1, PACK)):
                nc.vector.quantize_mx(
                    codes[:, t0:t1, :].rearrange("p t m -> p (t m)").bitcast(FP8X4),
                    scales[:, t0:t1, :].rearrange("p t m -> p (t m)"),
                    woven[:, t0:t1, :, :].rearrange("p t m j -> p (t m j)"),
                )
            return codes, scales

        nc.gpsimd.dma_start(unit_t[:], unit.rearrange("(p t) o -> p (t o)", t=PACK))
        w2_a = load_w("w2", w2, 0, 128, "slot_a")
        nc.sync.dma_start(offs_t[:], offs)
        nc.sync.dma_start(qry_t[:], qry)
        nc.sync.dma_start(prtn_t[:], prtn)
        w1_a = load_w("w1", w1, 0, 128, "slot_b")
        w2_b = load_w("w2", w2, 128, 256, "slot_c")
        w2_c = load_w("w2", w2, 256, 512, "slot_d")
        x_stab = load_scales("x_stab", x_scales, nc.vector, None)

        w2_woven = sb("w2_woven", [P, PACK, P, PACK], BF16)
        w1_woven = sb("w1_woven", [P, PACK, P, PACK], BF16)
        weave(w2_woven, w2_a, 0, nc.vector.tensor_copy)
        x_tab = load_words("x_tab", x_words, "slot_a")
        weave(w1_woven, w1_a, 0, nc.vector.tensor_copy)
        e_stab = load_scales("e_stab", e_scales, nc.vector, "slot_b")
        weave(w2_woven, w2_b, 128, nc.vector.tensor_copy)
        w1_b = load_w("w1", w1, 128, 384, "slot_c")
        weave(w2_woven, w2_c, 256, nc.scalar.copy)
        w1_c = load_w("w1", w1, 384, 512, "slot_d")

        x_s = sb("x_s", [P, S], U8)
        x_c = [sb("x_c%d" % h, [P, S // 2], U32) for h in range(2)]
        nc.vector.tensor_copy(x_s[:], x_stab[:].indirect(offs_t[:]))
        codes, scales = quant("w2", w2_woven)
        e_tab = load_words("e_tab", e_words, "w2_woven")
        for h in range(2):
            nc.vector.tensor_copy(x_c[h][:], x_tab[:].indirect(offs_t[:, 16 * h : 16 * (h + 1)]))
        ndw_tab = sb("ndw_tab", [P, T], F32, tag="slot_a")
        nc.sync.dma_start(ndw_tab[:], ndw)
        e_s = []

        def gather_e_scales(h, tag):
            part = sb("e_s%d" % h, [P, Z // 2], U8, tag=tag)
            nc.vector.tensor_copy(part[:], e_stab[:].indirect(qry_t[:, 16 * h : 16 * (h + 1)]))
            e_s.append(part)

        gather_e_scales(0, None)
        gates = []
        for t in range(PACK):
            bank = psum.tile([P, S], F32, name="g%d" % t, tag="g%d" % t)
            product(bank, codes[:, t, :], scales[:, t, :])
            gate = sb("gate%d" % t, [P, S], F32)
            nc.scalar.activation(gate[:], bank[:], ACT.Sigmoid)
            gates.append(gate[:])

        weave(w1_woven, w1_b, 128, nc.vector.tensor_copy)
        weave(w1_woven, w1_c, 384, nc.vector.tensor_copy)
        warm = sb("warm", [P, 1], F32)
        nc.scalar.activation(warm[:], gates[PACK - 1][:, 0:1], ACT.Abs_reciprocal_sqrt, bias=EPS, scale=1.0 / V)
        banks = []
        codes, scales = quant("w1", w1_woven)
        for t in range(PACK):
            bank = psum.tile([P, S], F32, name="y%d" % t, tag="y%d" % t)
            product(bank, codes[:, t, :], scales[:, t, :])
            banks.append(bank)

        gather_e_scales(1, "w1_woven")
        kept = sb("kept", [P, PACK, V], F32)
        hid = sb("hid", [P, PACK, V], BF16)
        gated = [sb("gated%d" % t, [P, V, 2], F32) for t in range(PACK)]

        def gate_mult(t):
            nc.vector.tensor_tensor(gated[t][:].rearrange("p v d -> p (v d)"), banks[t][:], gates[t], ALU.mult)

        ss = [sb("ss%d" % u, [P, 2], F32) for u in range(2)]
        rstd = [sb("rstd%d" % u, [P, 2], F32) for u in range(2)]

        def keep(t):
            nc.vector.tensor_tensor(kept[:, t, :], gated[t][:, :, 0], gated[t][:, :, 1], ALU.max)
            sq = sb("sq%d" % t, [P, V], F32, tag="sq")
            nc.scalar.activation(sq[:], kept[:, t, :], ACT.Square, accum_out=ss[t // 2][:, t % 2 : t % 2 + 1])

        def inverse_root(u):
            nc.scalar.activation(rstd[u][:], ss[u][:], ACT.Abs_reciprocal_sqrt, bias=EPS, scale=1.0 / V)

        gate_mult(0)
        gate_mult(1)
        keep(0)
        gate_mult(2)
        keep(1)
        inverse_root(0)
        fac = sb("fac", [P, 2], F32)
        nc.gpsimd.tensor_tensor(fac[:], rstd[0][:], unit_t[:, 0:2], ALU.mult)
        gate_mult(3)
        keep(2)
        keep(3)
        inverse_root(1)
        for t in range(2):
            nc.scalar.activation(hid[:, t, :], kept[:, t, :], ACT.Copy, scale=fac[:, t : t + 1])

        e_c = sb("e_c", [P, Z], U32, tag="gated%d" % (PACK - 1))
        nc.vector.tensor_copy(e_c[:], e_tab[:].indirect(qry_t[:]))
        for t in range(2, PACK):
            nc.vector.tensor_scalar(hid[:, t, :], kept[:, t, :], rstd[1][:, t - 2 : t - 1], unit_t[:, t : t + 1], ALU.mult, ALU.mult)
        wq = sb("wq", [P, Z], F32, tag="fac")
        nc.scalar.activation(wq[:], ndw_tab[:].indirect(qry_t[:]), ACT.Copy)

        NB = V // P
        HZ = Z // 2
        woven = []
        for b in range(NB):
            hw = sb("hid_woven%d" % b, [P, P, PACK], BF16)
            nc.vector.tensor_copy(
                hw[:].rearrange("p (c i) t -> p c t i", i=4),
                hid[:, :, b * P : (b + 1) * P].rearrange("p t (c i) -> p c t i", i=4),
            )
            woven.append(hw)
        banks = {}
        for b in range(NB):
            codes = sb("h_c%d" % b, [P, P], U32)
            scales = sb("h_s%d" % b, [P, P], U8)
            nc.vector.quantize_mx(codes[:].bitcast(FP8X4), scales[:], woven[b][:].rearrange("p v t -> p (v t)"))
            for h in range(2):
                cols = slice(h * HZ, (h + 1) * HZ)
                bank = psum.tile([P, HZ], F32, name="s%d%d" % (b, h), tag="g%d" % (2 * b + h))
                nc.tensor.matmul_mx(bank[:], codes[:].bitcast(FP8X4), scales[:], e_c[:, cols].bitcast(FP8X4), e_s[h][:], start=True, stop=True)
                banks[b, h] = bank

        scs = [sb("sc%d" % b, [P, Z], F32) for b in range(NB)]
        names = ("spar", "pen", "gap", "wgap", "res")
        tl = {(n, b, h): sb("%s%d%d" % (n, b, h), [P, HZ], F32) for n in names for b in range(NB) for h in range(2)}

        def half(h):
            return slice(h * HZ, (h + 1) * HZ)

        def drain(b, h, on_vector):
            if on_vector:
                nc.vector.tensor_copy(scs[b][:, half(h)], banks[b, h][:])
            else:
                nc.scalar.copy(scs[b][:, half(h)], banks[b, h][:])

        def fetch(b, h, on_vector):
            src = scs[b][:].indirect(prtn_t[:, h * (HZ // 16) : (h + 1) * (HZ // 16)])
            if on_vector:
                nc.vector.tensor_copy(tl["spar", b, h][:], src)
            else:
                nc.scalar.activation(tl["spar", b, h][:], src, ACT.Copy)

        def square(b, h):
            nc.scalar.activation(tl["pen", b, h][:], tl["spar", b, h][:], ACT.Square, scale=math.sqrt(PENALTY))

        def weigh(b, h):
            nc.vector.tensor_tensor(tl["gap", b, h][:], scs[b][:, half(h)], tl["spar", b, h][:], ALU.subtract)

        def weigh2(b, h):
            nc.vector.tensor_tensor(tl["wgap", b, h][:], tl["gap", b, h][:], wq[:, half(h)], ALU.mult)

        def finish(b, h):
            nc.vector.tensor_tensor(tl["res", b, h][:], tl["wgap", b, h][:], tl["pen", b, h][:], ALU.subtract)
            nc.sync.dma_start(out[b * P : (b + 1) * P, half(h)], tl["res", b, h][:])

        drain(0, 0, False)
        drain(0, 1, True)
        fetch(0, 1, True)
        fetch(0, 0, False)
        drain(1, 0, False)
        drain(1, 1, False)
        fetch(1, 1, False)
        square(0, 1)
        fetch(1, 0, False)
        square(0, 0)
        square(1, 1)
        square(1, 0)
        weigh(0, 1)
        weigh(0, 0)
        weigh2(0, 1)
        weigh2(0, 0)
        weigh(1, 1)
        finish(0, 1)
        weigh2(1, 1)
        weigh(1, 0)
        finish(0, 0)
        weigh2(1, 0)
        finish(1, 1)
        finish(1, 0)
